import numpy as np, ml_dtypes
CORES = [1,14,19,24,37,42,55,60,65,78,83,88,101,106,119,124]
N = 16
KB, QP = 2, 64
MEM = [1,7]
def setup_inputs(rng):
    return {"q": rng.standard_normal((N, 128, QP), dtype=np.float32).astype(ml_dtypes.bfloat16), "k": rng.standard_normal((N, 128, KB * 128), dtype=np.float32).astype(ml_dtypes.bfloat16), "v": rng.standard_normal((N, 128, KB * 128), dtype=np.float32).astype(ml_dtypes.bfloat16)}
def setup_inputs_big(rng):
    d = setup_inputs(rng)
    for k in ("q", "k", "v"): d[k] = (d[k].astype(np.float32) * 1024.0).astype(d[k].dtype)
    return d
def setup_inputs_small(rng):
    d = setup_inputs(rng)
    for k in ("q", "k", "v"): d[k] = (d[k].astype(np.float32) * (1 / 1024.0)).astype(d[k].dtype)
    return d
def setup_inputs_apart(rng):
    d = setup_inputs(rng)
    f = (10.0 ** rng.permutation(np.linspace(-1.5, 1.5, N))).astype(np.float32).reshape(N, 1, 1)
    for k in ("q", "k", "v"): d[k] = (d[k].astype(np.float32) * f).astype(d[k].dtype)
    return d
def reference(q, k, v):
    Q, K, V = q.astype(np.float64), k.astype(np.float64), v.astype(np.float64)
    y = np.zeros((N, 128, QP))
    for r in range(N):
        for j in MEM:
            for b in range(KB):
                S = np.maximum(K[j][:, 128 * b:128 * b + 128].T @ Q[r], 0.0)
                y[r] += V[j][:, 128 * b:128 * b + 128].T @ S
    return {"y": y.astype(ml_dtypes.bfloat16 if q.dtype != np.float64 else np.float64)}

@@ -1,0 +1,243 @@
+from concourse.bass import DstId, RemoteDMATransfer
+from concourse.mybir import AluOpType
+
+QP, KB, BK = 64, 2, 128
+KW = KB * BK
+GR, NG = 4, 2
+
+SCRATCH = {
+    "kq": ("sbuf", [128, KW + QP], "bfloat16"),
+    "vown": ("sbuf", [128, KW], "bfloat16"),
+    "land": ("sbuf", [128, KW + GR * NG * QP], "bfloat16"),
+    "vrem": ("sbuf", [128, KW], "bfloat16"),
+    "zero": ("sbuf", [128, KB * GR * QP], "float32"),
+    "o": ("sbuf", [128, GR * NG * QP], "bfloat16"),
+    "qd": ("dram", [128, QP], "bfloat16"),
+    "qf": ("dram", [128, QP], "bfloat16"),
+    "yl": ("dram", [128, QP], "bfloat16"),
+}
+SEMAPHORES = ["kl", "vl", "kr", "vr", "zs", "ld", "fa", "ya", "st", "sent"]
+for _g in range(NG):
+    SCRATCH["pa%d" % _g] = ("psum", [128, 512], "float32")
+    SCRATCH["pb%d" % _g] = ("psum", [128, 512], "float32")
+    SCRATCH["po%d" % _g] = ("psum", [128, 512], "float32")
+    SCRATCH["s%d" % _g] = ("sbuf", [128, 2 * KB * GR * QP], "bfloat16")
+    SEMAPHORES += [n + "%d" % _g for n in ("qa", "ma", "mb", "ra", "rb", "mo", "cp")]
+
+
+def _engines(topo, src, dst):
+    m = topo.mask(src, dst)
+    return [i for i in range(m.bit_length()) if (m >> i) & 1]
+
+
+def _bits(es):
+    b = 0
+    for i in es:
+        b |= 1 << i
+    return b
+
+
+def _spread(es, n):
+    return es[::len(es) // n][:n]
+
+
+def _plan(T, topo):
+    cores, mem = list(T.cores), list(T.tables["MEM"])
+    n, site = len(cores), [cores[j] for j in mem]
+    ns = len(site)
+    ok = [[m for m in range(ns) if cores[r] == site[m] or topo.may_write(site[m], cores[r])] for r in range(n)]
+    serve, load = [None] * n, [0] * ns
+    for r in range(n):
+        if len(ok[r]) == 1:
+            serve[r] = ok[r][0]
+            load[serve[r]] += 1
+    for r in range(n):
+        if serve[r] is None:
+            serve[r] = min(ok[r], key=lambda m: (load[m], m))
+            load[serve[r]] += 1
+    via, used = [None] * n, []
+    for r in range(n):
+        s = site[serve[r]]
+        if cores[r] == s or topo.may_write(cores[r], s):
+            continue
+        c = [f for f in range(n) if f not in used and f not in mem and serve[f] == serve[r]
+             and topo.may_write(cores[f], s) and topo.same_plane(topo.chip(cores[r]), topo.chip(cores[f]))]
+        c.sort(key=lambda f: (topo.die(cores[f]) != topo.die(cores[r]), f))
+        via[r] = c[0]
+        used.append(c[0])
+    order = []
+    for m in range(ns):
+        mine = [r for r in range(n) if serve[r] == m]
+        rider = [r for r in mine if r in mem and r != mem[m]]
+        own = [r for r in mine if r == mem[m]]
+        direct = [r for r in mine if via[r] is None and r not in mem]
+        late = [r for r in mine if via[r] is not None]
+        order.append(rider + direct + own + late)
+    return cores, mem, site, serve, via, order
+
+
+def rank_program(g, core, T, topo):
+    rank = T.rank_of(core)
+    if rank is None:
+        return
+    cores, mem, site, serve, via, order = _plan(T, topo)
+    sem = T.sem
+    sent = [0]
+
+    def send(dst, out_ap, in_ap, rsem, es):
+        rid, pid, _ = topo.addr(dst)
+        g.remote_dma(out_ap, in_ap, rsem, sem.sent, pid, rid, _bits(es))
+        sent[0] += len(es)
+
+    def q_engines(r):
+        src = cores[r] if via[r] is None else cores[via[r]]
+        es = _engines(topo, src, site[serve[r]])
+        fwd = via[r] is not None or r in via
+        return es if fwd else _spread(es, len(es) // 2)
+
+    def groups(m):
+        return [order[m][i:i + GR] for i in range(0, len(order[m]), GR)]
+
+    def ret_engines(m, grp):
+        rem = [r for r in grp if cores[r] != site[m]]
+        out = {}
+        for t, r in enumerate(rem):
+            es = _engines(topo, site[m], cores[r])
+            per = 1
+            while per * 2 * len(rem) <= len(es):
+                per *= 2
+            out[r] = es[t * per:(t + 1) * per]
+        return out
+
+    my = serve[rank]
+    slot = order[my].index(rank)
+    is_site = rank in mem
+
+    if not is_site:
+        g.sync.dma_start(T.qd[:, :], T.q[:, :]).then_inc(sem.ld, 16)
+        g.wait_ge(sem.ld, 16)
+        if via[rank] is None:
+            send(site[my], T.land[:, KW + slot * QP:KW + (slot + 1) * QP], T.qd[:, :],
+                 sem["qa%d" % (slot // GR)], q_engines(rank))
+        else:
+            f = cores[via[rank]]
+            send(f, T.qf[:, :], T.qd[:, :], sem.fa, _spread(_engines(topo, core, f), 2))
+        if rank in via:
+            p = via.index(rank)
+            ps = order[my].index(p)
+            g.wait_ge(sem.fa, 2)
+            send(site[my], T.land[:, KW + ps * QP:KW + (ps + 1) * QP], T.qf[:, :],
+                 sem["qa%d" % (ps // GR)], q_engines(p))
+        g.wait_ge(sem.sent, sent[0])
+
+    if is_site:
+        m = mem.index(rank)
+        peer = site[1 - m]
+        rides = my != m
+        grps = groups(m)
+        has_rider = order[m][0] in mem and order[m][0] != rank
+        g.sync.dma_start(T.kq[:, 0:KW], T.k[:, :]).then_inc(sem.kl, 16)
+        nkl = 16
+        if rides:
+            g.scalar.dma_start(T.kq[:, KW:KW + QP], T.q[:, :]).then_inc(sem.kl, 16)
+            nkl = 32
+        else:
+            g.scalar.dma_start(T.land[:, KW + slot * QP:KW + (slot + 1) * QP], T.q[:, :]).then_inc(
+                sem["qa%d" % (slot // GR)], 16)
+        g.scalar.dma_start(T.vown[:, :], T.v[:, :]).then_inc(sem.vl, 16)
+        ex = _engines(topo, core, peer)
+        w = KW + QP if rides else KW
+        g.wait_ge(sem.kl, nkl)
+        send(peer, T.land[:, 0:w], T.kq[:, 0:w], sem.kr, ex)
+        g.wait_ge(sem.vl, 16)
+        send(peer, T.vrem[:, :], T.vown[:, :], sem.vr, ex)
+        nex = len(_engines(topo, peer, core))
+
+        te, ve = g.tensor, g.vector
+        ve.memset(T.zero[:, :], 0.0).then_inc(sem.zs, 1)
+        ve.wait_ge(sem.zs, 1)
+
+        def cols(i):
+            return len(grps[i]) * QP
+
+        def m1(i):
+            nq = sum(len(q_engines(r)) for r in grps[i] if r not in mem) + (16 if rank in grps[i] else 0)
+            c0, nc = KW + i * GR * QP, cols(i)
+            te.wait_ge(sem.kl, nkl)
+            if nq:
+                te.wait_ge(sem["qa%d" % i], nq)
+            if has_rider and i == 0:
+                te.wait_ge(sem.kr, nex)
+            for b in range(KB):
+                te.matmul(out=T["pa%d" % i][:, b * nc:(b + 1) * nc], lhsT=T.kq[:, b * BK:(b + 1) * BK],
+                          rhs=T.land[:, c0:c0 + nc], start=True, stop=True).then_inc(sem["ma%d" % i], 1)
+            te.wait_ge(sem.kr, nex)
+            for b in range(KB):
+                te.matmul(out=T["pb%d" % i][:, b * nc:(b + 1) * nc], lhsT=T.land[:, b * BK:(b + 1) * BK],
+                          rhs=T.land[:, c0:c0 + nc], start=True, stop=True).then_inc(sem["mb%d" % i], 1)
+
+        def m2(i, remote):
+            nc = cols(i)
+            te.wait_ge(sem.vr if remote else sem.vl, nex if remote else 16)
+            te.wait_ge(sem[("rb%d" if remote else "ra%d") % i], 1)
+            v = T.vrem if remote else T.vown
+            off = KB * nc if remote else 0
+            for b in range(KB):
+                te.matmul(out=T["po%d" % i][:, 0:nc], lhsT=v[:, b * BK:(b + 1) * BK],
+                          rhs=T["s%d" % i][:, off + b * nc:off + (b + 1) * nc],
+                          start=(not remote and b == 0), stop=(remote and b == KB - 1)).then_inc(sem["mo%d" % i], 1)
+
+        def relu(i):
+            wd = KB * cols(i)
+            for p, ms, rs, off in (("pa%d", "ma%d", "ra%d", 0), ("pb%d", "mb%d", "rb%d", wd)):
+                ve.wait_ge(sem[ms % i], KB)
+                ve.tensor_tensor(out=T["s%d" % i][:, off:off + wd], in0=T[p % i][:, 0:wd], in1=T.zero[:, 0:wd],
+                                 op=AluOpType.max).then_inc(sem[rs % i], 1)
+
+        def copy(i):
+            nc = cols(i)
+            ve.wait_ge(sem["mo%d" % i], 2 * KB)
+            ve.tensor_copy(out=T.o[:, i * GR * QP:i * GR * QP + nc], in_=T["po%d" % i][:, 0:nc]).then_inc(
+                sem["cp%d" % i], 1)
+
+        early = [i for i in range(len(grps)) if all(via[r] is None for r in grps[i])]
+        late = [i for i in range(len(grps)) if i not in early]
+        for i in early:
+            m1(i)
+            relu(i)
+        for i in early:
+            m2(i, False)
+        for i in early:
+            m2(i, True)
+            copy(i)
+        for i in late:
+            m1(i)
+            relu(i)
+            m2(i, False)
+            m2(i, True)
+            copy(i)
+
+        for i in early + late:
+            g.wait_ge(sem["cp%d" % i], 1)
+            re = ret_engines(m, grps[i])
+            tr = []
+            for r in grps[i]:
+                if r not in re:
+                    continue
+                rid, pid, _ = topo.addr(cores[r])
+                sl = order[m].index(r)
+                tr.append(RemoteDMATransfer(dst_ids=[DstId(rid=rid, pnc=pid)], dma_engine_mask=_bits(re[r]),
+                                            remote_sem=sem.ya, src=T.o[:, sl * QP:(sl + 1) * QP], dst=T.yl[:, :]))
+                sent[0] += len(re[r])
+            if tr:
+                g.remote_dma_fused(tr, local_sem=sem.sent)
+        g.wait_ge(sem.sent, sent[0])
+
+    if core == site[my]:
+        g.sync.wait_ge(sem["cp%d" % (slot // GR)], 1)
+        g.sync.dma_start(T.y[:, :], T.o[:, slot * QP:(slot + 1) * QP]).then_inc(sem.st, 16)
+    else:
+        grp = groups(my)[slot // GR]
+        g.sync.wait_ge(sem.ya, len(ret_engines(my, grp)[rank]))
+        g.sync.dma_start(T.y[:, :], T.yl[:, :]).then_inc(sem.st, 16)
+    g.sync.wait_ge(sem.st, 16)

@@ -1,28 +1,29 @@
 from concourse.bass import DstId, RemoteDMATransfer
-from concourse.mybir import AluOpType
+from concourse.mybir import AluOpType, ActivationFunctionType
 
 QP, KB, BK = 64, 2, 128
 KW = KB * BK
-GR, NG = 4, 2
+PR, NP = 2, 2
+NH = PR * NP - 1
 
 SCRATCH = {
-    "kq": ("sbuf", [128, KW + QP], "bfloat16"),
-    "vown": ("sbuf", [128, KW], "bfloat16"),
-    "land": ("sbuf", [128, KW + GR * NG * QP], "bfloat16"),
-    "vrem": ("sbuf", [128, KW], "bfloat16"),
-    "zero": ("sbuf", [128, KB * GR * QP], "float32"),
-    "o": ("sbuf", [128, GR * NG * QP], "bfloat16"),
+    "kb": ("sbuf", [128, KW], "bfloat16"),
+    "vb": ("sbuf", [128, KW], "bfloat16"),
+    "land": ("sbuf", [128, PR * NP * QP], "bfloat16"),
+    "o": ("sbuf", [128, PR * NP * QP], "bfloat16"),
+    "y0": ("sbuf", [128, QP], "bfloat16"),
+    "y1": ("sbuf", [128, QP], "bfloat16"),
+    "ys": ("sbuf", [128, QP], "bfloat16"),
     "qd": ("dram", [128, QP], "bfloat16"),
     "qf": ("dram", [128, QP], "bfloat16"),
-    "yl": ("dram", [128, QP], "bfloat16"),
 }
-SEMAPHORES = ["kl", "vl", "kr", "vr", "zs", "ld", "fa", "ya", "st", "sent"]
-for _g in range(NG):
-    SCRATCH["pa%d" % _g] = ("psum", [128, 512], "float32")
-    SCRATCH["pb%d" % _g] = ("psum", [128, 512], "float32")
-    SCRATCH["po%d" % _g] = ("psum", [128, 512], "float32")
-    SCRATCH["s%d" % _g] = ("sbuf", [128, 2 * KB * GR * QP], "bfloat16")
-    SEMAPHORES += [n + "%d" % _g for n in ("qa", "ma", "mb", "ra", "rb", "mo", "cp")]
+SEMAPHORES = ["ks", "vs", "qo", "ld", "fa", "ya", "ad", "st", "sent"]
+for _p in range(NP):
+    SCRATCH["pa%d" % _p] = ("psum", [128, 512], "float32")
+    SCRATCH["pb%d" % _p] = ("psum", [128, 512], "float32")
+    SCRATCH["po%d" % _p] = ("psum", [128, 512], "float32")
+    SCRATCH["s%d" % _p] = ("sbuf", [128, KB * PR * QP], "bfloat16")
+    SEMAPHORES += [n + "%d" % _p for n in ("q", "ma", "mb", "ra", "rb", "mo", "cp")]
 
 
 def _engines(topo, src, dst):
@@ -37,207 +38,196 @@ def _bits(es):
     return b
 
 
-def _spread(es, n):
-    return es[::len(es) // n][:n]
-
-
 def _plan(T, topo):
     cores, mem = list(T.cores), list(T.tables["MEM"])
-    n, site = len(cores), [cores[j] for j in mem]
-    ns = len(site)
-    ok = [[m for m in range(ns) if cores[r] == site[m] or topo.may_write(site[m], cores[r])] for r in range(n)]
-    serve, load = [None] * n, [0] * ns
-    for r in range(n):
-        if len(ok[r]) == 1:
-            serve[r] = ok[r][0]
-            load[serve[r]] += 1
-    for r in range(n):
-        if serve[r] is None:
-            serve[r] = min(ok[r], key=lambda m: (load[m], m))
-            load[serve[r]] += 1
+    n, nm = len(cores), len(mem)
+    everyone = range(topo.CHIPS * topo.CORES_PER_CHIP)
+    sites = []
+    for j in mem:
+        mc = cores[j]
+        free = [c for c in everyone if topo.chip(c) == topo.chip(mc) and c not in cores
+                and all(topo.may_write(c, x) for x in cores)]
+        same = [c for c in free if topo.die(c) == topo.die(mc)]
+        other = [c for c in free if topo.die(c) != topo.die(mc)]
+        k = (NH + 1) // 2 - 1
+        sites.append([mc] + same[:k] + other[:NH - k])
+    flat = [s for ss in sites for s in ss]
     via, used = [None] * n, []
     for r in range(n):
-        s = site[serve[r]]
-        if cores[r] == s or topo.may_write(cores[r], s):
+        if all(cores[r] == s or topo.may_write(cores[r], s) for s in flat):
             continue
-        c = [f for f in range(n) if f not in used and f not in mem and serve[f] == serve[r]
-             and topo.may_write(cores[f], s) and topo.same_plane(topo.chip(cores[r]), topo.chip(cores[f]))]
+        c = [f for f in range(n) if f not in used and f not in mem
+             and all(topo.may_write(cores[f], s) for s in flat)
+             and topo.same_plane(topo.chip(cores[r]), topo.chip(cores[f]))]
         c.sort(key=lambda f: (topo.die(cores[f]) != topo.die(cores[r]), f))
         via[r] = c[0]
         used.append(c[0])
-    order = []
-    for m in range(ns):
-        mine = [r for r in range(n) if serve[r] == m]
-        rider = [r for r in mine if r in mem and r != mem[m]]
-        own = [r for r in mine if r == mem[m]]
-        direct = [r for r in mine if via[r] is None and r not in mem]
-        late = [r for r in mine if via[r] is not None]
-        order.append(rider + direct + own + late)
-    return cores, mem, site, serve, via, order
+    member, where = [], []
+    cap = PR * NP
+    for m in range(nm):
+        mb = {s: [] for s in sites[m]}
+        mb[sites[m][0]].append(mem[m])
+        ok = {r: [s for s in sites[m] if topo.may_write(s, cores[r])] for r in range(n) if r != mem[m]}
+        for r in sorted(ok, key=lambda r: (len(ok[r]), r)):
+            late = via[r] is not None
+            s = min([s for s in ok[r] if len(mb[s]) < cap],
+                    key=lambda s: (sum(1 for x in mb[s] if via[x] is not None) if late else 0,
+                                   topo.die(s) != topo.die(cores[r]), len(mb[s]), s))
+            mb[s].append(r)
+        wh = {}
+        for s in mb:
+            mb[s].sort(key=lambda r: (via[r] is not None, r in mem and cores[r] != s, cores[r] != s, r))
+            for i, r in enumerate(mb[s]):
+                wh[r] = (s, i)
+        member.append(mb)
+        where.append(wh)
+    return cores, mem, sites, member, where, via
 
 
 def rank_program(g, core, T, topo):
+    cores, mem, sites, member, where, via = _plan(T, topo)
     rank = T.rank_of(core)
-    if rank is None:
+    sm = [m for m in range(len(mem)) if core in sites[m]]
+    if rank is None and not sm:
         return
-    cores, mem, site, serve, via, order = _plan(T, topo)
     sem = T.sem
     sent = [0]
+    te, ve, se = g.tensor, g.vector, g.scalar
 
-    def send(dst, out_ap, in_ap, rsem, es):
+    def tr(dst, dst_ap, src_ap, rsem, es):
         rid, pid, _ = topo.addr(dst)
-        g.remote_dma(out_ap, in_ap, rsem, sem.sent, pid, rid, _bits(es))
         sent[0] += len(es)
+        return RemoteDMATransfer(dst_ids=[DstId(rid=rid, pnc=pid)], dma_engine_mask=_bits(es), remote_sem=rsem,
+                                 src=src_ap, dst=dst_ap)
 
     def q_engines(r):
         src = cores[r] if via[r] is None else cores[via[r]]
-        es = _engines(topo, src, site[serve[r]])
-        fwd = via[r] is not None or r in via
-        return es if fwd else _spread(es, len(es) // 2)
-
-    def groups(m):
-        return [order[m][i:i + GR] for i in range(0, len(order[m]), GR)]
-
-    def ret_engines(m, grp):
-        rem = [r for r in grp if cores[r] != site[m]]
+        dst = [m for m in range(len(mem)) if where[m][r][0] != cores[r]]
         out = {}
-        for t, r in enumerate(rem):
-            es = _engines(topo, site[m], cores[r])
-            per = 1
-            while per * 2 * len(rem) <= len(es):
-                per *= 2
-            out[r] = es[t * per:(t + 1) * per]
+        for t, m in enumerate(dst):
+            es = _engines(topo, src, where[m][r][0])
+            per = len(es) // len(dst)
+            out[m] = es[t * per:(t + 1) * per]
         return out
 
-    my = serve[rank]
-    slot = order[my].index(rank)
-    is_site = rank in mem
+    def send_q(r, src_ap):
+        qe = q_engines(r)
+        g.remote_dma_fused([tr(where[m][r][0], T.land[:, where[m][r][1] * QP:(where[m][r][1] + 1) * QP], src_ap,
+                               sem["q%d" % (where[m][r][1] // PR)], qe[m]) for m in qe], local_sem=sem.sent)
 
-    if not is_site:
+    def ret_engines(m, r):
+        s, slot = where[m][r]
+        piece = member[m][s][slot // PR * PR:(slot // PR + 1) * PR]
+        rem = [x for x in piece if cores[x] != s]
+        es = _engines(topo, s, cores[r])
+        per = 1
+        while per * 2 * len(rem) <= len(es):
+            per *= 2
+        t = rem.index(r)
+        return es[t * per:(t + 1) * per]
+
+    if rank is not None and not sm:
         g.sync.dma_start(T.qd[:, :], T.q[:, :]).then_inc(sem.ld, 16)
         g.wait_ge(sem.ld, 16)
         if via[rank] is None:
-            send(site[my], T.land[:, KW + slot * QP:KW + (slot + 1) * QP], T.qd[:, :],
-                 sem["qa%d" % (slot // GR)], q_engines(rank))
+            send_q(rank, T.qd[:, :])
         else:
             f = cores[via[rank]]
-            send(f, T.qf[:, :], T.qd[:, :], sem.fa, _spread(_engines(topo, core, f), 2))
+            es = _engines(topo, core, f)
+            es = es[::len(es) // 2][:2]
+            rid, pid, _ = topo.addr(f)
+            g.remote_dma(T.qf[:, :], T.qd[:, :], sem.fa, sem.sent, pid, rid, _bits(es))
+            sent[0] += len(es)
         if rank in via:
-            p = via.index(rank)
-            ps = order[my].index(p)
             g.wait_ge(sem.fa, 2)
-            send(site[my], T.land[:, KW + ps * QP:KW + (ps + 1) * QP], T.qf[:, :],
-                 sem["qa%d" % (ps // GR)], q_engines(p))
+            send_q(via.index(rank), T.qf[:, :])
         g.wait_ge(sem.sent, sent[0])
 
-    if is_site:
-        m = mem.index(rank)
-        peer = site[1 - m]
-        rides = my != m
-        grps = groups(m)
-        has_rider = order[m][0] in mem and order[m][0] != rank
-        g.sync.dma_start(T.kq[:, 0:KW], T.k[:, :]).then_inc(sem.kl, 16)
-        nkl = 16
-        if rides:
-            g.scalar.dma_start(T.kq[:, KW:KW + QP], T.q[:, :]).then_inc(sem.kl, 16)
-            nkl = 32
+    if sm:
+        m = sm[0]
+        mc = sites[m][0]
+        mine = member[m][core]
+        nkv = 16
+        if core == mc:
+            slot = where[m][rank][1]
+            g.sync.dma_start(T.kb[:, :], T.k[:, :]).then_inc(sem.ks, 16)
+            g.scalar.dma_start(T.land[:, slot * QP:(slot + 1) * QP], T.q[:, :]).then_inc(sem.qo, 16)
+            g.scalar.dma_start(T.vb[:, :], T.v[:, :]).then_inc(sem.vs, 16)
+            g.wait_ge(sem.qo, 16)
+            send_q(rank, T.land[:, slot * QP:(slot + 1) * QP])
+            hs = sites[m][1:]
+            es = [e for e in _engines(topo, core, hs[0]) if all(e in _engines(topo, core, h) for h in hs)]
+            ids = [DstId(rid=topo.addr(h)[0], pnc=topo.addr(h)[1]) for h in hs]
+            for buf, s in ((T.kb, sem.ks), (T.vb, sem.vs)):
+                g.wait_ge(s, 16)
+                g.remote_dma_fused([RemoteDMATransfer(dst_ids=ids, dma_engine_mask=_bits(es), remote_sem=s,
+                                                      srcs=[buf[:, :]], dsts=[buf[:, :] for _ in hs])],
+                                   local_sem=sem.sent)
+                sent[0] += len(es)
         else:
-            g.scalar.dma_start(T.land[:, KW + slot * QP:KW + (slot + 1) * QP], T.q[:, :]).then_inc(
-                sem["qa%d" % (slot // GR)], 16)
-        g.scalar.dma_start(T.vown[:, :], T.v[:, :]).then_inc(sem.vl, 16)
-        ex = _engines(topo, core, peer)
-        w = KW + QP if rides else KW
-        g.wait_ge(sem.kl, nkl)
-        send(peer, T.land[:, 0:w], T.kq[:, 0:w], sem.kr, ex)
-        g.wait_ge(sem.vl, 16)
-        send(peer, T.vrem[:, :], T.vown[:, :], sem.vr, ex)
-        nex = len(_engines(topo, peer, core))
+            hs = sites[m][1:]
+            nkv = len([e for e in _engines(topo, mc, hs[0]) if all(e in _engines(topo, mc, h) for h in hs)])
 
-        te, ve = g.tensor, g.vector
-        ve.memset(T.zero[:, :], 0.0).then_inc(sem.zs, 1)
-        ve.wait_ge(sem.zs, 1)
+        nc = PR * QP
 
-        def cols(i):
-            return len(grps[i]) * QP
-
-        def m1(i):
-            nq = sum(len(q_engines(r)) for r in grps[i] if r not in mem) + (16 if rank in grps[i] else 0)
-            c0, nc = KW + i * GR * QP, cols(i)
-            te.wait_ge(sem.kl, nkl)
+        def m1(p):
+            piece = mine[p * PR:(p + 1) * PR]
+            nq = sum(len(q_engines(r)[m]) for r in piece if cores[r] != core)
+            te.wait_ge(sem.ks, nkv)
             if nq:
-                te.wait_ge(sem["qa%d" % i], nq)
-            if has_rider and i == 0:
-                te.wait_ge(sem.kr, nex)
-            for b in range(KB):
-                te.matmul(out=T["pa%d" % i][:, b * nc:(b + 1) * nc], lhsT=T.kq[:, b * BK:(b + 1) * BK],
-                          rhs=T.land[:, c0:c0 + nc], start=True, stop=True).then_inc(sem["ma%d" % i], 1)
-            te.wait_ge(sem.kr, nex)
-            for b in range(KB):
-                te.matmul(out=T["pb%d" % i][:, b * nc:(b + 1) * nc], lhsT=T.land[:, b * BK:(b + 1) * BK],
-                          rhs=T.land[:, c0:c0 + nc], start=True, stop=True).then_inc(sem["mb%d" % i], 1)
+                te.wait_ge(sem["q%d" % p], nq)
+            if any(cores[r] == core for r in piece):
+                te.wait_ge(sem.qo, 16)
+            for b, (ps, ms) in enumerate((("pa%d", "ma%d"), ("pb%d", "mb%d"))):
+                te.matmul(out=T[ps % p][:, 0:nc], lhsT=T.kb[:, b * BK:(b + 1) * BK],
+                          rhs=T.land[:, p * nc:(p + 1) * nc], start=True, stop=True).then_inc(sem[ms % p], 1)
+            ve.wait_ge(sem["ma%d" % p], 1)
+            ve.tensor_scalar(out=T["s%d" % p][:, 0:nc], in0=T["pa%d" % p][:, 0:nc], scalar1=0.0, scalar2=None,
+                             op0=AluOpType.max).then_inc(sem["ra%d" % p], 1)
+            se.wait_ge(sem["mb%d" % p], 1)
+            se.activation(out=T["s%d" % p][:, nc:2 * nc], in_=T["pb%d" % p][:, 0:nc],
+                          func=ActivationFunctionType.Relu).then_inc(sem["rb%d" % p], 1)
 
-        def m2(i, remote):
-            nc = cols(i)
-            te.wait_ge(sem.vr if remote else sem.vl, nex if remote else 16)
-            te.wait_ge(sem[("rb%d" if remote else "ra%d") % i], 1)
-            v = T.vrem if remote else T.vown
-            off = KB * nc if remote else 0
-            for b in range(KB):
-                te.matmul(out=T["po%d" % i][:, 0:nc], lhsT=v[:, b * BK:(b + 1) * BK],
-                          rhs=T["s%d" % i][:, off + b * nc:off + (b + 1) * nc],
-                          start=(not remote and b == 0), stop=(remote and b == KB - 1)).then_inc(sem["mo%d" % i], 1)
+        def m2(p):
+            te.wait_ge(sem.vs, nkv)
+            for b, rs in enumerate(("ra%d", "rb%d")):
+                te.wait_ge(sem[rs % p], 1)
+                te.matmul(out=T["po%d" % p][:, 0:nc], lhsT=T.vb[:, b * BK:(b + 1) * BK],
+                          rhs=T["s%d" % p][:, b * nc:(b + 1) * nc],
+                          start=(b == 0), stop=(b == KB - 1)).then_inc(sem["mo%d" % p], 1)
+            ve.wait_ge(sem["mo%d" % p], KB)
+            ve.tensor_copy(out=T.o[:, p * nc:(p + 1) * nc], in_=T["po%d" % p][:, 0:nc]).then_inc(sem["cp%d" % p], 1)
 
-        def relu(i):
-            wd = KB * cols(i)
-            for p, ms, rs, off in (("pa%d", "ma%d", "ra%d", 0), ("pb%d", "mb%d", "rb%d", wd)):
-                ve.wait_ge(sem[ms % i], KB)
-                ve.tensor_tensor(out=T["s%d" % i][:, off:off + wd], in0=T[p % i][:, 0:wd], in1=T.zero[:, 0:wd],
-                                 op=AluOpType.max).then_inc(sem[rs % i], 1)
+        if any(via[r] is not None for r in mine):
+            for p in range(NP):
+                m1(p)
+                m2(p)
+        else:
+            for p in range(NP):
+                m1(p)
+            for p in range(NP):
+                m2(p)
 
-        def copy(i):
-            nc = cols(i)
-            ve.wait_ge(sem["mo%d" % i], 2 * KB)
-            ve.tensor_copy(out=T.o[:, i * GR * QP:i * GR * QP + nc], in_=T["po%d" % i][:, 0:nc]).then_inc(
-                sem["cp%d" % i], 1)
-
-        early = [i for i in range(len(grps)) if all(via[r] is None for r in grps[i])]
-        late = [i for i in range(len(grps)) if i not in early]
-        for i in early:
-            m1(i)
-            relu(i)
-        for i in early:
-            m2(i, False)
-        for i in early:
-            m2(i, True)
-            copy(i)
-        for i in late:
-            m1(i)
-            relu(i)
-            m2(i, False)
-            m2(i, True)
-            copy(i)
-
-        for i in early + late:
-            g.wait_ge(sem["cp%d" % i], 1)
-            re = ret_engines(m, grps[i])
-            tr = []
-            for r in grps[i]:
-                if r not in re:
-                    continue
-                rid, pid, _ = topo.addr(cores[r])
-                sl = order[m].index(r)
-                tr.append(RemoteDMATransfer(dst_ids=[DstId(rid=rid, pnc=pid)], dma_engine_mask=_bits(re[r]),
-                                            remote_sem=sem.ya, src=T.o[:, sl * QP:(sl + 1) * QP], dst=T.yl[:, :]))
-                sent[0] += len(re[r])
-            if tr:
-                g.remote_dma_fused(tr, local_sem=sem.sent)
+        for p in range(NP):
+            g.wait_ge(sem["cp%d" % p], 1)
+            lst = [tr(cores[r], T["y%d" % m][:, :], T.o[:, where[m][r][1] * QP:(where[m][r][1] + 1) * QP], sem.ya,
+                      ret_engines(m, r)) for r in mine[p * PR:(p + 1) * PR] if cores[r] != core]
+            if lst:
+                g.remote_dma_fused(lst, local_sem=sem.sent)
         g.wait_ge(sem.sent, sent[0])
 
-    if core == site[my]:
-        g.sync.wait_ge(sem["cp%d" % (slot // GR)], 1)
-        g.sync.dma_start(T.y[:, :], T.o[:, slot * QP:(slot + 1) * QP]).then_inc(sem.st, 16)
-    else:
-        grp = groups(my)[slot // GR]
-        g.sync.wait_ge(sem.ya, len(ret_engines(my, grp)[rank]))
-        g.sync.dma_start(T.y[:, :], T.yl[:, :]).then_inc(sem.st, 16)
-    g.sync.wait_ge(sem.st, 16)
+    if rank is not None:
+        parts, nya = [], 0
+        for m in range(len(mem)):
+            s, slot = where[m][rank]
+            if s == core:
+                ve.wait_ge(sem["cp%d" % (slot // PR)], 1)
+                parts.append(T.o[:, slot * QP:(slot + 1) * QP])
+            else:
+                nya += len(ret_engines(m, rank))
+                parts.append(T["y%d" % m][:, :])
+        ve.wait_ge(sem.ya, nya)
+        ve.tensor_tensor(out=T.ys[:, :], in0=parts[0], in1=parts[1], op=AluOpType.add).then_inc(sem.ad, 1)
+        g.sync.wait_ge(sem.ad, 1)
+        g.sync.dma_start(T.y[:, :], T.ys[:, :]).then_inc(sem.st, 16)
+        g.sync.wait_ge(sem.st, 16)

from concourse.bass import DstId, RemoteDMATransfer
from concourse.mybir import AluOpType, ActivationFunctionType

QP, KB, BK = 64, 2, 128
KW = KB * BK
PR, NP = 2, 2
NH = PR * NP - 1

SCRATCH = {
    "kb": ("sbuf", [128, KW], "bfloat16"),
    "vb": ("sbuf", [128, KW], "bfloat16"),
    "land": ("sbuf", [128, PR * NP * QP], "bfloat16"),
    "o": ("sbuf", [128, PR * NP * QP], "bfloat16"),
    "y0": ("sbuf", [128, QP], "bfloat16"),
    "y1": ("sbuf", [128, QP], "bfloat16"),
    "ys": ("sbuf", [128, QP], "bfloat16"),
    "qd": ("dram", [128, QP], "bfloat16"),
    "qf": ("dram", [128, QP], "bfloat16"),
}
SEMAPHORES = ["ks", "vs", "qo", "ld", "fa", "ya", "ad", "st", "sent"]
for _p in range(NP):
    SCRATCH["pa%d" % _p] = ("psum", [128, 512], "float32")
    SCRATCH["pb%d" % _p] = ("psum", [128, 512], "float32")
    SCRATCH["po%d" % _p] = ("psum", [128, 512], "float32")
    SCRATCH["s%d" % _p] = ("sbuf", [128, KB * PR * QP], "bfloat16")
    SEMAPHORES += [n + "%d" % _p for n in ("q", "ma", "mb", "ra", "rb", "mo", "cp")]


def _engines(topo, src, dst):
    m = topo.mask(src, dst)
    return [i for i in range(m.bit_length()) if (m >> i) & 1]


def _bits(es):
    b = 0
    for i in es:
        b |= 1 << i
    return b


def _plan(T, topo):
    cores, mem = list(T.cores), list(T.tables["MEM"])
    n, nm = len(cores), len(mem)
    everyone = range(topo.CHIPS * topo.CORES_PER_CHIP)
    sites = []
    for j in mem:
        mc = cores[j]
        free = [c for c in everyone if topo.chip(c) == topo.chip(mc) and c not in cores
                and all(topo.may_write(c, x) for x in cores)]
        same = [c for c in free if topo.die(c) == topo.die(mc)]
        other = [c for c in free if topo.die(c) != topo.die(mc)]
        k = (NH + 1) // 2 - 1
        sites.append([mc] + same[:k] + other[:NH - k])
    flat = [s for ss in sites for s in ss]
    via, used = [None] * n, []
    for r in range(n):
        if all(cores[r] == s or topo.may_write(cores[r], s) for s in flat):
            continue
        c = [f for f in range(n) if f not in used and f not in mem
             and all(topo.may_write(cores[f], s) for s in flat)
             and topo.same_plane(topo.chip(cores[r]), topo.chip(cores[f]))]
        c.sort(key=lambda f: (topo.die(cores[f]) != topo.die(cores[r]), f))
        via[r] = c[0]
        used.append(c[0])
    member, where = [], []
    cap = PR * NP
    for m in range(nm):
        mb = {s: [] for s in sites[m]}
        mb[sites[m][0]].append(mem[m])
        ok = {r: [s for s in sites[m] if topo.may_write(s, cores[r])] for r in range(n) if r != mem[m]}
        for r in sorted(ok, key=lambda r: (len(ok[r]), r)):
            late = via[r] is not None
            s = min([s for s in ok[r] if len(mb[s]) < cap],
                    key=lambda s: (sum(1 for x in mb[s] if via[x] is not None) if late else 0,
                                   topo.die(s) != topo.die(cores[r]), len(mb[s]), s))
            mb[s].append(r)
        wh = {}
        for s in mb:
            mb[s].sort(key=lambda r: (via[r] is not None, r in mem and cores[r] != s, cores[r] != s, r))
            for i, r in enumerate(mb[s]):
                wh[r] = (s, i)
        member.append(mb)
        where.append(wh)
    return cores, mem, sites, member, where, via


def rank_program(g, core, T, topo):
    cores, mem, sites, member, where, via = _plan(T, topo)
    rank = T.rank_of(core)
    sm = [m for m in range(len(mem)) if core in sites[m]]
    if rank is None and not sm:
        return
    sem = T.sem
    sent = [0]
    te, ve, se = g.tensor, g.vector, g.scalar

    def tr(dst, dst_ap, src_ap, rsem, es):
        rid, pid, _ = topo.addr(dst)
        sent[0] += len(es)
        return RemoteDMATransfer(dst_ids=[DstId(rid=rid, pnc=pid)], dma_engine_mask=_bits(es), remote_sem=rsem,
                                 src=src_ap, dst=dst_ap)

    def q_engines(r):
        src = cores[r] if via[r] is None else cores[via[r]]
        dst = [m for m in range(len(mem)) if where[m][r][0] != cores[r]]
        out = {}
        for t, m in enumerate(dst):
            es = _engines(topo, src, where[m][r][0])
            per = len(es) // len(dst)
            out[m] = es[t * per:(t + 1) * per]
        return out

    def send_q(r, src_ap):
        qe = q_engines(r)
        g.remote_dma_fused([tr(where[m][r][0], T.land[:, where[m][r][1] * QP:(where[m][r][1] + 1) * QP], src_ap,
                               sem["q%d" % (where[m][r][1] // PR)], qe[m]) for m in qe], local_sem=sem.sent)

    def ret_engines(m, r):
        s, slot = where[m][r]
        piece = member[m][s][slot // PR * PR:(slot // PR + 1) * PR]
        rem = [x for x in piece if cores[x] != s]
        es = _engines(topo, s, cores[r])
        per = 1
        while per * 2 * len(rem) <= len(es):
            per *= 2
        t = rem.index(r)
        return es[t * per:(t + 1) * per]

    if rank is not None and not sm:
        g.sync.dma_start(T.qd[:, :], T.q[:, :]).then_inc(sem.ld, 16)
        g.wait_ge(sem.ld, 16)
        if via[rank] is None:
            send_q(rank, T.qd[:, :])
        else:
            f = cores[via[rank]]
            es = _engines(topo, core, f)
            es = es[::len(es) // 2][:2]
            rid, pid, _ = topo.addr(f)
            g.remote_dma(T.qf[:, :], T.qd[:, :], sem.fa, sem.sent, pid, rid, _bits(es))
            sent[0] += len(es)
        if rank in via:
            g.wait_ge(sem.fa, 2)
            send_q(via.index(rank), T.qf[:, :])
        g.wait_ge(sem.sent, sent[0])

    if sm:
        m = sm[0]
        mc = sites[m][0]
        mine = member[m][core]
        nkv = 16
        if core == mc:
            slot = where[m][rank][1]
            g.sync.dma_start(T.kb[:, :], T.k[:, :]).then_inc(sem.ks, 16)
            g.scalar.dma_start(T.land[:, slot * QP:(slot + 1) * QP], T.q[:, :]).then_inc(sem.qo, 16)
            g.scalar.dma_start(T.vb[:, :], T.v[:, :]).then_inc(sem.vs, 16)
            g.wait_ge(sem.qo, 16)
            send_q(rank, T.land[:, slot * QP:(slot + 1) * QP])
            hs = sites[m][1:]
            es = [e for e in _engines(topo, core, hs[0]) if all(e in _engines(topo, core, h) for h in hs)]
            ids = [DstId(rid=topo.addr(h)[0], pnc=topo.addr(h)[1]) for h in hs]
            for buf, s in ((T.kb, sem.ks), (T.vb, sem.vs)):
                g.wait_ge(s, 16)
                g.remote_dma_fused([RemoteDMATransfer(dst_ids=ids, dma_engine_mask=_bits(es), remote_sem=s,
                                                      srcs=[buf[:, :]], dsts=[buf[:, :] for _ in hs])],
                                   local_sem=sem.sent)
                sent[0] += len(es)
        else:
            hs = sites[m][1:]
            nkv = len([e for e in _engines(topo, mc, hs[0]) if all(e in _engines(topo, mc, h) for h in hs)])

        nc = PR * QP

        def m1(p):
            piece = mine[p * PR:(p + 1) * PR]
            nq = sum(len(q_engines(r)[m]) for r in piece if cores[r] != core)
            te.wait_ge(sem.ks, nkv)
            if nq:
                te.wait_ge(sem["q%d" % p], nq)
            if any(cores[r] == core for r in piece):
                te.wait_ge(sem.qo, 16)
            for b, (ps, ms) in enumerate((("pa%d", "ma%d"), ("pb%d", "mb%d"))):
                te.matmul(out=T[ps % p][:, 0:nc], lhsT=T.kb[:, b * BK:(b + 1) * BK],
                          rhs=T.land[:, p * nc:(p + 1) * nc], start=True, stop=True).then_inc(sem[ms % p], 1)
            ve.wait_ge(sem["ma%d" % p], 1)
            ve.tensor_scalar(out=T["s%d" % p][:, 0:nc], in0=T["pa%d" % p][:, 0:nc], scalar1=0.0, scalar2=None,
                             op0=AluOpType.max).then_inc(sem["ra%d" % p], 1)
            se.wait_ge(sem["mb%d" % p], 1)
            se.activation(out=T["s%d" % p][:, nc:2 * nc], in_=T["pb%d" % p][:, 0:nc],
                          func=ActivationFunctionType.Relu).then_inc(sem["rb%d" % p], 1)

        def m2(p):
            te.wait_ge(sem.vs, nkv)
            for b, rs in enumerate(("ra%d", "rb%d")):
                te.wait_ge(sem[rs % p], 1)
                te.matmul(out=T["po%d" % p][:, 0:nc], lhsT=T.vb[:, b * BK:(b + 1) * BK],
                          rhs=T["s%d" % p][:, b * nc:(b + 1) * nc],
                          start=(b == 0), stop=(b == KB - 1)).then_inc(sem["mo%d" % p], 1)
            ve.wait_ge(sem["mo%d" % p], KB)
            ve.tensor_copy(out=T.o[:, p * nc:(p + 1) * nc], in_=T["po%d" % p][:, 0:nc]).then_inc(sem["cp%d" % p], 1)

        if any(via[r] is not None for r in mine):
            for p in range(NP):
                m1(p)
                m2(p)
        else:
            for p in range(NP):
                m1(p)
            for p in range(NP):
                m2(p)

        for p in range(NP):
            g.wait_ge(sem["cp%d" % p], 1)
            lst = [tr(cores[r], T["y%d" % m][:, :], T.o[:, where[m][r][1] * QP:(where[m][r][1] + 1) * QP], sem.ya,
                      ret_engines(m, r)) for r in mine[p * PR:(p + 1) * PR] if cores[r] != core]
            if lst:
                g.remote_dma_fused(lst, local_sem=sem.sent)
        g.wait_ge(sem.sent, sent[0])

    if rank is not None:
        parts, nya = [], 0
        for m in range(len(mem)):
            s, slot = where[m][rank]
            if s == core:
                ve.wait_ge(sem["cp%d" % (slot // PR)], 1)
                parts.append(T.o[:, slot * QP:(slot + 1) * QP])
            else:
                nya += len(ret_engines(m, rank))
                parts.append(T["y%d" % m][:, :])
        ve.wait_ge(sem.ya, nya)
        ve.tensor_tensor(out=T.ys[:, :], in0=parts[0], in1=parts[1], op=AluOpType.add).then_inc(sem.ad, 1)
        g.sync.wait_ge(sem.ad, 1)
        g.sync.dma_start(T.y[:, :], T.ys[:, :]).then_inc(sem.st, 16)
        g.sync.wait_ge(sem.st, 16)
